import numpy as np
import ml_dtypes


def mxq(x, axis, fmt="e4m3"):
    dtype, down = {"e4m3": (ml_dtypes.float8_e4m3fn, 7), "e5m2": (ml_dtypes.float8_e5m2, 14)}[fmt]
    v = np.moveaxis(np.asarray(x, np.float32).astype(ml_dtypes.bfloat16).astype(np.float64), axis, -1)
    blocks = v.reshape(v.shape[:-1] + (-1, 32))
    amax = np.abs(blocks).max(-1, keepdims=True)
    byte = np.maximum(np.where(amax > 0, np.frexp(amax)[1] - 1 + 127, 0) - down, 1)
    scale = np.exp2(byte - 127.0)
    codes = (blocks / scale).astype(np.float32).astype(dtype).astype(np.float64)
    return np.moveaxis((codes * scale).reshape(v.shape), -1, axis)


WIDE = False


def mx_kscale(k):
    if not WIDE:
        return np.ones(k)
    levels = np.array([10, -10, 5, -5, 0])
    if k % 512:
        return np.exp2(np.random.permutation(np.resize(levels, k // 32))).repeat(32)
    a = np.empty((k // 512, 16))
    for p in range(k // 512):
        a[p, :8] = np.random.permutation(np.resize(levels, 8))
        for g in range(8):
            far = levels[np.abs(levels - a[p, g]) >= 10]
            a[p, g + 8] = far[np.random.randint(len(far))]
    return np.exp2(a.ravel()).repeat(32)


def f64(x):
    return np.asarray(x).astype(np.float64)


def striped(idx):
    return np.tile(idx.reshape(-1, 16).T, (8, 1)).astype(np.uint16)


def unstriped(offs):
    return offs[:16].T.reshape(-1).astype(np.int64)


E2M1 = np.array([0.0, 0.5, 1.0, 1.5, 2.0, 3.0, 4.0, 6.0, -0.0, -0.5, -1.0, -1.5, -2.0, -3.0, -4.0, -6.0])


def pack_weight(w, fmt):
    k, n = w.shape
    w = f64(np.asarray(w, np.float32).astype(ml_dtypes.bfloat16)).reshape(k // 32, 32, n)
    amax = np.abs(w).max(1)
    if fmt == "e4m3":
        byte = np.frexp(amax)[1] - 1 + 127 - 7
    else:
        mant, ex = np.frexp(amax / 6.0)
        byte = np.where(mant > 0.5, ex, ex - 1) + 127
    byte = np.clip(np.where(amax > 0, byte, 1), 1, 254)
    scaled = (w * np.exp2(127.0 - byte)[:, None, :]).reshape(k, n).astype(np.float32)
    by_word = np.ascontiguousarray(scaled.reshape(k // 512, 128, 4, n).transpose(0, 1, 3, 2))
    if fmt == "e4m3":
        words = by_word.astype(ml_dtypes.float8_e4m3fn).view(np.uint8)
    else:
        c = by_word.astype(ml_dtypes.float4_e2m1fn).view(np.uint8) & 0xF
        words = (c[..., 0::2] | (c[..., 1::2] << 4)).reshape(k // 512, 128, 2 * n)
    return np.ascontiguousarray(words), np.ascontiguousarray(byte.astype(np.uint8).reshape(k // 512, 16, n))


def unpack_weight(words, scales, fmt):
    g, _, n = scales.shape
    words = np.ascontiguousarray(words).reshape(g, 128, n, -1)
    if fmt == "e4m3":
        vals = words.view(ml_dtypes.float8_e4m3fn).astype(np.float64)
    else:
        nib = np.empty((g, 128, n, 4), np.uint8)
        nib[..., 0::2] = words & 0xF
        nib[..., 1::2] = words >> 4
        vals = E2M1[nib]
    vals = vals * np.repeat(np.exp2(scales.astype(np.float64) - 127.0), 8, axis=1)[..., None]
    return vals.transpose(0, 1, 3, 2).reshape(g * 512, n)


def gelu(v):
    return 0.5 * v * (1.0 + np.tanh(np.sqrt(2.0 / np.pi) * (v + 0.044715 * v**3)))


K, K2, H, N, T, S = 1536, 1024, 512, 384, 4096, 1024


def setup_inputs():
    n = np.random.standard_normal
    s = mx_kscale(K)[:, None]
    s2 = mx_kscale(K2)[:, None]
    u = mx_kscale(H)[:, None]
    d = {}
    d["tab_words"], d["tab_scales"] = pack_weight(n((K, T)) * s, "e4m3")
    d["offs"] = striped(np.random.permutation(T)[:S])
    d["xs_words"], d["xs_scales"] = pack_weight(n((K2, S)) * s2, "e4m3")
    d["wa"] = (1.6 * n((K, H)) / K**0.5 / s).astype(np.float32)
    d["wb_words"], d["wb_scales"] = pack_weight(1.6 * n((K, H)) / K**0.5 / s, "e2m1")
    d["gain"] = (np.exp(0.3 * n(H)) * u[:, 0]).astype(np.float32)
    d["ws"] = (1.2 * n((K2, H)) / K2**0.5 / s2 * u.T).astype(np.float32)
    d["wo_words"], d["wo_scales"] = pack_weight(1.8 * n((H, N)) / H**0.5 / u, "e2m1")
    return d


def reference(tab_words, tab_scales, offs, xs_words, xs_scales, wa, wb_words, wb_scales, gain, ws, wo_words, wo_scales):
    v = unpack_weight(tab_words, tab_scales, "e4m3")[:, unstriped(offs)]
    xs = unpack_weight(xs_words, xs_scales, "e4m3")
    wb = unpack_weight(wb_words, wb_scales, "e2m1")
    wo = unpack_weight(wo_words, wo_scales, "e2m1")
    left = np.tanh(mxq(f64(wa), 0, "e4m3").T @ v)
    right = np.tanh(wb.T @ v)
    apart = np.abs(left - right) * f64(gain)[:, None]
    seen = mxq(f64(ws), 0, "e4m3").T @ xs
    h = mxq(np.maximum(apart, seen), 0, "e4m3")
    y = wo.T @ h
    return 1.0 / (1.0 + np.exp(-y))

from contextlib import ExitStack

import concourse.mybir as mybir

K, K2, H, N, T, S = 1536, 1024, 512, 384, 4096, 1024
FLOPS = 2 * S * (2 * K * H + K2 * H + H * N)

F32 = mybir.dt.float32
BF16 = mybir.dt.bfloat16
I32 = mybir.dt.int32
U32 = mybir.dt.uint32
U16 = mybir.dt.uint16
U8 = mybir.dt.uint8
FP8X4 = mybir.dt.float8_e4m3fn_x4
FP4X4 = mybir.dt.float4_e2m1fn_x4
ACT = mybir.ActivationFunctionType
ALU = mybir.AluOpType

P = 128
PACK = 4
KP = P * PACK
PASSES = K // KP
PASSES2 = K2 // KP
HALF = 512
HALVES = S // HALF
SHIFT_ROWS = 112


def tile_list_parcel_conflict_score_kernel(
    tc, tab_words, tab_scales, offs, xs_words, xs_scales, wa, wb_words, wb_scales, gain, ws, wo_words, wo_scales, out
):
    nc = tc.nc
    with ExitStack() as ctx:
        keep = ctx.enter_context(tc.tile_pool(name="keep", bufs=1))
        ring = ctx.enter_context(tc.tile_pool(name="ring", bufs=3))
        stage = ctx.enter_context(tc.tile_pool(name="stage", bufs=1))
        psum = ctx.enter_context(tc.psum_pool(name="psum", bufs=1))

        def held(name, shape, dtype):
            return keep.tile(shape, dtype, name=name, align_bytes=64)

        def staged(name, shape, dtype, kib):
            return stage.tile(shape, dtype, name=name, align_bytes=64, offset=int(kib * 1024))

        def bank(b, name):
            return psum.tile([P, HALF], F32, name=name, tag="bank%d" % b)

        def load_table(a, kib):
            words = staged("tab%d" % a, [P, T], I32, kib)
            nc.sync.dma_start(words[:], tab_words[a].rearrange("p t i -> p (t i)").bitcast(I32))
            return words

        def load_rows(w, name, a, kib):
            raw = staged("%s_raw%d" % (name, a), [P, PACK, H], F32, kib)
            nc.sync.dma_start(raw[:], w[a * KP : (a + 1) * KP, :].rearrange("(p j) c -> p j c", j=PACK))
            return raw

        offsets = keep.tile([P, S // 16], U16, name="offsets")
        nc.sync.dma_start(offsets[:], offs)
        wb_raw = held("wb_raw", [P, PASSES, 2 * H], U8)
        nc.sync.dma_start(wb_raw[:].bitcast(I32), wb_words.rearrange("a p n -> p a n").bitcast(I32))
        tab = [load_table(0, 0), load_table(1, 32)]

        tab_sc = staged("tab_sc", [P, T], U8, 64)
        nc.vector.memset(tab_sc[:].bitcast(I32), 0)
        for q in range(4):
            nc.gpsimd.dma_start(
                tab_sc[32 * q : 32 * q + 4 * PASSES, :].bitcast(I32), tab_scales[:, 4 * q : 4 * q + 4, :].bitcast(I32)
            )
        wb_sc_raw = staged("wb_sc_raw", [P, PASSES, H], U8, 55)
        nc.vector.memset(wb_sc_raw[:].bitcast(I32), 0)
        for q in range(4):
            nc.scalar.dma_start(
                wb_sc_raw[32 * q : 32 * q + 4, :, :].bitcast(I32),
                wb_scales[:, 4 * q : 4 * q + 4, :].rearrange("a r n -> r a n").bitcast(I32),
            )
        xs_sc = held("xs_sc", [P, S], U8)
        nc.vector.memset(xs_sc[:].bitcast(I32), 0)
        wo_sc = held("wo_sc", [P, N], U8)
        nc.vector.memset(wo_sc[:].bitcast(I32), 0)
        for q in range(4):
            nc.scalar.dma_start(
                xs_sc[32 * q : 32 * q + 4 * PASSES2, :].bitcast(I32), xs_scales[:, 4 * q : 4 * q + 4, :].bitcast(I32)
            )
        for q in range(4):
            nc.scalar.dma_start(wo_sc[32 * q : 32 * q + 4, :].bitcast(I32), wo_scales[0, 4 * q : 4 * q + 4, :].bitcast(I32))
        wo = held("wo", [P, 2 * N], U8)
        nc.sync.dma_start(wo[:].bitcast(I32), wo_words[0].bitcast(I32))
        gains = held("gains", [P, PACK], F32)
        nc.sync.dma_start(gains[:], gain.rearrange("(p t) -> p t", t=PACK))

        warm = held("warm", [P, 2], F32)
        nc.vector.memset(warm[:, 0:1], 0.0)
        nc.scalar.activation(warm[:, 1:2], warm[:, 0:1], ACT.Sigmoid)

        wb = []
        for a in range(PASSES):
            wb.append(held("wb%d" % a, [P, 2 * H], U8))
            nc.vector.tensor_copy(
                wb[a][:].rearrange("p (t m b) -> p t m b", t=PACK, b=2),
                wb_raw[:, a, :].rearrange("p (m t b) -> p t m b", t=PACK, b=2),
            )

        v = [held("v0", [P, S], U32)]
        nc.vector.tensor_copy(v[0][:], tab[0][:].bitcast(U32).indirect(offsets[:]))
        tab.append(load_table(2, 8))

        v_sc0 = held("v_sc0", [P, S], U8)
        nc.vector.tensor_copy(v_sc0[:], tab_sc[:].indirect(offsets[:]))
        v_sc = [v_sc0]
        for a in range(1, PASSES):
            v_sc.append(held("v_sc%d" % a, [P, S], U8))
            nc.vector.memset(v_sc[a][96:128, :].bitcast(I32), 0)
            nc.scalar.dma_start(v_sc[a][0:SHIFT_ROWS, :].bitcast(I32), v_sc0[4 * a : 4 * a + SHIFT_ROWS, :].bitcast(I32))

        wb_sc = held("wb_sc", [P, PASSES, H], U8)
        nc.vector.tensor_copy(
            wb_sc[:].rearrange("p a (t m) -> p a t m", t=PACK),
            wb_sc_raw[:].rearrange("p a (m t) -> p a t m", t=PACK),
        )
        wa_raw = [load_rows(wa, "wa", 0, 48), load_rows(wa, "wa", 1, 56)]

        v.append(staged("v1", [P, S], U32, 64))
        nc.vector.tensor_copy(v[1][:], tab[1][:].bitcast(U32).indirect(offsets[:]))
        wa_raw.append(load_rows(wa, "wa", 2, 32))
        ws_raw = [load_rows(ws, "ws", 0, 40)]

        v.append(held("v2", [P, S], U32))
        for h in range(HALVES):
            picks = offsets[:, h * (HALF // 16) : (h + 1) * (HALF // 16)]
            nc.vector.tensor_copy(v[2][:, h * HALF : (h + 1) * HALF], tab[2][:].bitcast(U32).indirect(picks))
        ws_raw.append(load_rows(ws, "ws", 1, 8))
        xs = []
        for h in range(HALVES):
            xs.append(staged("xs%d" % h, [P, PASSES2, HALF], I32, 16 + 4 * h))
            cols = xs_words[:, :, h * HALF : (h + 1) * HALF, :]
            nc.sync.dma_start(xs[h][:], cols.rearrange("a p c i -> p a (c i)").bitcast(I32))

        units = [(h, t) for h in range(HALVES) for t in range(PACK)]
        right = {}
        for a in range(PASSES):
            for h, t in units:
                if a == 0:
                    right[h, t] = bank(PACK * h + t, "right%d_%d" % (h, t))
                nc.tensor.matmul_mx(
                    right[h, t][:],
                    lhsT=wb[a][:, 2 * P * t : 2 * P * (t + 1)].bitcast(FP4X4),
                    lhsT_scale=wb_sc[:, a, P * t : P * (t + 1)],
                    rhs=v[a][:, h * HALF : (h + 1) * HALF].bitcast(FP8X4),
                    rhs_scale=v_sc[a][:, h * HALF : (h + 1) * HALF],
                    start=(a == 0),
                    stop=(a == PASSES - 1),
                )
        tb = {}
        for h, t in units:
            tb[h, t] = held("tb%d_%d" % (h, t), [P, HALF], F32)
            nc.scalar.activation(tb[h, t][:], right[h, t][:], ACT.Tanh)

        def quantised_weight(raw, name):
            grouped = ring.tile([P, PACK * H], BF16, name="grouped", align_bytes=64)
            nc.vector.tensor_copy(
                grouped[:].rearrange("p (t m j) -> p m j t", t=PACK, j=PACK),
                raw[:].rearrange("p j (m t) -> p m j t", t=PACK),
            )
            codes = held(name + "_codes", [P, H], U32)
            scales = held(name + "_scales", [P, H], U8)
            nc.vector.quantize_mx(codes[:].bitcast(FP8X4), scales[:], grouped[:])
            return codes, scales

        left = {}
        for a in range(PASSES):
            codes, scales = quantised_weight(wa_raw[a], "wa%d" % a)
            for h, t in units:
                if a == 0:
                    left[h, t] = bank(PACK * h + t, "left%d_%d" % (h, t))
                nc.tensor.matmul_mx(
                    left[h, t][:],
                    lhsT=codes[:, P * t : P * (t + 1)].bitcast(FP8X4),
                    lhsT_scale=scales[:, P * t : P * (t + 1)],
                    rhs=v[a][:, h * HALF : (h + 1) * HALF].bitcast(FP8X4),
                    rhs_scale=v_sc[a][:, h * HALF : (h + 1) * HALF],
                    start=(a == 0),
                    stop=(a == PASSES - 1),
                )

        dist = {}
        for h, t in units:
            ta = ring.tile([P, HALF], F32, name="ta")
            nc.scalar.activation(ta[:], left[h, t][:], ACT.Tanh)
            diff = ring.tile([P, HALF], F32, name="diff")
            nc.vector.tensor_tensor(diff[:], ta[:], tb[h, t][:], ALU.subtract)
            dist[h, t] = held("dist%d_%d" % (h, t), [P, HALF], F32)
            nc.scalar.activation(dist[h, t][:], diff[:], ACT.Abs)

        wsq = [quantised_weight(ws_raw[a], "ws%d" % a) for a in range(PASSES2)]
        for h in range(HALVES):
            planes = held("planes%d" % h, [P, PACK, HALF], BF16)
            for t in range(PACK):
                seen = bank(PACK * h + t, "seen%d_%d" % (h, t))
                for a in range(PASSES2):
                    nc.tensor.matmul_mx(
                        seen[:],
                        lhsT=wsq[a][0][:, P * t : P * (t + 1)].bitcast(FP8X4),
                        lhsT_scale=wsq[a][1][:, P * t : P * (t + 1)],
                        rhs=xs[h][:, a, :].bitcast(FP8X4),
                        rhs_scale=xs_sc[4 * a : P, h * HALF : (h + 1) * HALF],
                        start=(a == 0),
                        stop=(a == PASSES2 - 1),
                    )
                nc.vector.scalar_tensor_tensor(
                    planes[:, t, :], dist[h, t][:], gains[:, t : t + 1], seen[:], ALU.mult, ALU.max
                )
            woven = held("woven%d" % h, [P, HALF * PACK], BF16)
            nc.vector.tensor_copy(
                woven[:].rearrange("p (c i t) -> p c t i", i=4, t=PACK),
                planes[:].rearrange("p t (c i) -> p c t i", i=4),
            )
            h_codes = held("h_codes%d" % h, [P, HALF], U32)
            h_scales = held("h_scales%d" % h, [P, HALF], U8)
            nc.vector.quantize_mx(h_codes[:].bitcast(FP8X4), h_scales[:], woven[:])
            for n in range(N // P):
                y = bank(PACK * h + n, "y%d_%d" % (h, n))
                nc.tensor.matmul_mx(
                    y[:],
                    lhsT=wo[:, 2 * P * n : 2 * P * (n + 1)].bitcast(FP4X4),
                    lhsT_scale=wo_sc[:, P * n : P * (n + 1)],
                    rhs=h_codes[:].bitcast(FP8X4),
                    rhs_scale=h_scales[:],
                    start=True,
                    stop=True,
                )
                score = held("score%d_%d" % (h, n), [P, HALF], F32)
                nc.scalar.activation(score[:], y[:], ACT.Sigmoid)
                nc.sync.dma_start(out[P * n : P * (n + 1), h * HALF : (h + 1) * HALF], score[:])
